import numpy as np
import ml_dtypes


def mxq(x, axis, fmt="e4m3"):
    dtype, down = {"e4m3": (ml_dtypes.float8_e4m3fn, 7), "e5m2": (ml_dtypes.float8_e5m2, 14)}[fmt]
    v = np.moveaxis(np.asarray(x, np.float32).astype(ml_dtypes.bfloat16).astype(np.float64), axis, -1)
    blocks = v.reshape(v.shape[:-1] + (-1, 32))
    amax = np.abs(blocks).max(-1, keepdims=True)
    byte = np.maximum(np.where(amax > 0, np.frexp(amax)[1] - 1 + 127, 0) - down, 1)
    scale = np.exp2(byte - 127.0)
    codes = (blocks / scale).astype(np.float32).astype(dtype).astype(np.float64)
    return np.moveaxis((codes * scale).reshape(v.shape), -1, axis)


WIDE = False


def mx_kscale(k):
    if not WIDE:
        return np.ones(k)
    levels = np.array([10, -10, 5, -5, 0])
    if k % 512:
        return np.exp2(np.random.permutation(np.resize(levels, k // 32))).repeat(32)
    a = np.empty((k // 512, 16))
    for p in range(k // 512):
        a[p, :8] = np.random.permutation(np.resize(levels, 8))
        for g in range(8):
            far = levels[np.abs(levels - a[p, g]) >= 10]
            a[p, g + 8] = far[np.random.randint(len(far))]
    return np.exp2(a.ravel()).repeat(32)


def f64(x):
    return np.asarray(x).astype(np.float64)


def striped(idx):
    return np.tile(idx.reshape(-1, 16).T, (8, 1)).astype(np.uint16)


def unstriped(offs):
    return offs[:16].T.reshape(-1).astype(np.int64)


E2M1 = np.array([0.0, 0.5, 1.0, 1.5, 2.0, 3.0, 4.0, 6.0, -0.0, -0.5, -1.0, -1.5, -2.0, -3.0, -4.0, -6.0])


def pack_weight(w, fmt):
    k, n = w.shape
    w = f64(np.asarray(w, np.float32).astype(ml_dtypes.bfloat16)).reshape(k // 32, 32, n)
    amax = np.abs(w).max(1)
    if fmt == "e4m3":
        byte = np.frexp(amax)[1] - 1 + 127 - 7
    else:
        mant, ex = np.frexp(amax / 6.0)
        byte = np.where(mant > 0.5, ex, ex - 1) + 127
    byte = np.clip(np.where(amax > 0, byte, 1), 1, 254)
    scaled = (w * np.exp2(127.0 - byte)[:, None, :]).reshape(k, n).astype(np.float32)
    by_word = np.ascontiguousarray(scaled.reshape(k // 512, 128, 4, n).transpose(0, 1, 3, 2))
    if fmt == "e4m3":
        words = by_word.astype(ml_dtypes.float8_e4m3fn).view(np.uint8)
    else:
        c = by_word.astype(ml_dtypes.float4_e2m1fn).view(np.uint8) & 0xF
        words = (c[..., 0::2] | (c[..., 1::2] << 4)).reshape(k // 512, 128, 2 * n)
    return np.ascontiguousarray(words), np.ascontiguousarray(byte.astype(np.uint8).reshape(k // 512, 16, n))


def unpack_weight(words, scales, fmt):
    g, _, n = scales.shape
    words = np.ascontiguousarray(words).reshape(g, 128, n, -1)
    if fmt == "e4m3":
        vals = words.view(ml_dtypes.float8_e4m3fn).astype(np.float64)
    else:
        nib = np.empty((g, 128, n, 4), np.uint8)
        nib[..., 0::2] = words & 0xF
        nib[..., 1::2] = words >> 4
        vals = E2M1[nib]
    vals = vals * np.repeat(np.exp2(scales.astype(np.float64) - 127.0), 8, axis=1)[..., None]
    return vals.transpose(0, 1, 3, 2).reshape(g * 512, n)


def gelu(v):
    return 0.5 * v * (1.0 + np.tanh(np.sqrt(2.0 / np.pi) * (v + 0.044715 * v**3)))


def bf(x):
    return np.asarray(x, np.float32).astype(ml_dtypes.bfloat16)


def planes(Y):
    n, m = Y.shape
    b = f64(bf(Y)).reshape(n // 32, 32, m)
    amax = np.abs(b).max(1)
    byte = np.clip(np.where(amax > 0, np.frexp(amax)[1] - 1 + 127 - 7, 1), 1, 254)
    codes = (b * np.exp2(127.0 - byte)[:, None, :]).reshape(n, m).astype(np.float32).astype(ml_dtypes.float8_e4m3fn).view(np.uint8)
    words = codes.reshape(n // 512, 128, 4, m).transpose(0, 1, 3, 2)
    return np.ascontiguousarray(words), np.ascontiguousarray(byte.astype(np.uint8).reshape(n // 512, 16, m))


K, H, N, T, S, P = 1024, 512, 1024, 2048, 1024, 512


def setup_inputs():
    n = np.random.standard_normal
    s = mx_kscale(K)[:, None]
    u = mx_kscale(H)[:, None]
    tab_words, tab_scales = pack_weight(n((K, T)) * s, "e4m3")
    w2_words, w2_scales = pack_weight(n((K, H)) / np.sqrt(K) / s * u.T, "e2m1")
    return {
        "tab_words": tab_words,
        "tab_scales": tab_scales,
        "offs": striped(np.random.permutation(T)[:S]),
        "pos1": striped(np.random.permutation(S)[:P]),
        "pos2": striped(np.random.permutation(S)[:P]),
        "w1": (n((K, H)) / np.sqrt(K) / s * u.T).astype(np.float32),
        "w2_words": w2_words,
        "w2_scales": w2_scales,
        "motion": (0.8 * n((H, S))).astype(np.float32),
        "wa": (0.6 * n((H, N)) / np.sqrt(H) / u).astype(np.float32),
        "temp": np.random.uniform(0.4, 1.6, N).astype(np.float32),
        "signs": (4.0 * n((N, P))).astype(np.float32),
        "gain": np.exp(0.8 * n(N)).astype(np.float32),
    }


def reference(tab_words, tab_scales, offs, pos1, pos2, w1, w2_words, w2_scales, motion, wa, temp, signs, gain):
    v = unpack_weight(tab_words, tab_scales, "e4m3")[:, unstriped(offs)]
    w2 = unpack_weight(w2_words, w2_scales, "e2m1")
    h = (w2.T @ v) * f64(motion) + (mxq(f64(w1), 0, "e4m3").T @ v)
    e = mxq(f64(wa), 0, "e4m3").T @ mxq(h, 0, "e4m3")
    top = e.max(axis=1)
    a = np.exp(f64(temp)[:, None] * (e[:, unstriped(pos1)] - top[:, None])) * f64(signs)
    c = e[:, unstriped(pos2)]
    y = np.minimum(a, c) * f64(gain)[:, None]
    words, scales = planes(y)
    return y, words, scales

@@ -1,0 +1,280 @@
+from contextlib import ExitStack
+
+import concourse.mybir as mybir
+
+K, H, N, T, S, M = 1024, 512, 1024, 2048, 1024, 512
+FLOPS = 2 * (2 * K * H * S + H * N * S)
+
+F32 = mybir.dt.float32
+BF16 = mybir.dt.bfloat16
+I32 = mybir.dt.int32
+U32 = mybir.dt.uint32
+U16 = mybir.dt.uint16
+U8 = mybir.dt.uint8
+FP8X4 = mybir.dt.float8_e4m3fn_x4
+FP4X4 = mybir.dt.float4_e2m1fn_x4
+ALU = mybir.AluOpType
+ACT = mybir.ActivationFunctionType
+
+P = 128
+PACK = 4
+GROUP = P * PACK
+BANK = 512
+QUADS = 4
+
+
+def tile_list_stream_membership_page_kernel(
+    tc, tab_words, tab_scales, offs, pos1, pos2, w1, w2_words, w2_scales, motion, wa, temp, signs, gain,
+    out_0, out_1, out_2,
+):
+    nc = tc.nc
+    passes = K // GROUP
+    groups = N // GROUP
+    halves = S // BANK
+
+    with ExitStack() as ctx:
+        keep = ctx.enter_context(tc.tile_pool(name="keep", bufs=1))
+        ring = ctx.enter_context(tc.tile_pool(name="ring", bufs=3))
+        psum = ctx.enter_context(tc.psum_pool(name="psum", bufs=8))
+
+        def held(shape, dtype, name):
+            return keep.tile(shape, dtype, name=name, align_bytes=64)
+
+        scale_win = held([P, passes, T], U8, "scale_win")
+        nc.vector.memset(scale_win[:].bitcast(I32), 0)
+        w2s_raw = held([P, passes, H], U8, "w2s_raw")
+        nc.gpsimd.memset(w2s_raw[:].bitcast(I32), 0)
+
+        offs_sb = held([P, S // 16], U16, "offs_sb")
+        nc.sync.dma_start(offs_sb[:], offs)
+        for q in range(QUADS):
+            nc.scalar.dma_start(
+                out=scale_win[32 * q : 32 * q + 4, :, :].bitcast(I32),
+                in_=tab_scales[:, 4 * q : 4 * q + 4, :].rearrange("a r t -> r a t").bitcast(I32),
+            )
+        word_win = []
+        for a in range(passes):
+            win = held([P, T], U32, "word_win%d" % a)
+            nc.sync.dma_start(out=win[:].bitcast(I32), in_=tab_words[a].rearrange("p t i -> p (t i)").bitcast(I32))
+            word_win.append(win)
+        w2w_raw = held([P, passes, 2 * H], U8, "w2w_raw")
+        nc.sync.dma_start(out=w2w_raw[:].bitcast(I32), in_=w2_words.rearrange("a p b -> p a b").bitcast(I32))
+        for q in range(QUADS):
+            nc.scalar.dma_start(
+                out=w2s_raw[32 * q : 32 * q + 4, :, :].bitcast(I32),
+                in_=w2_scales[:, 4 * q : 4 * q + 4, :].rearrange("a r c -> r a c").bitcast(I32),
+            )
+        w1_raw = []
+        for a in range(passes):
+            raw = held([P, PACK, H], F32, "w1_raw%d" % a)
+            nc.sync.dma_start(out=raw[:], in_=w1[a * GROUP : (a + 1) * GROUP, :].rearrange("(p i) c -> p i c", i=PACK))
+            w1_raw.append(raw)
+        motion_rows = motion.rearrange("(p t) j -> p t j", t=PACK)
+        motion_sb = []
+        for t in range(PACK):
+            rows = held([P, S], F32, "motion%d" % t)
+            nc.sync.dma_start(out=rows[:], in_=motion_rows[:, t, :])
+            motion_sb.append(rows)
+        wa_rows = wa.rearrange("(p i) n -> p i n", i=PACK)
+        wa_raw = []
+        for g in range(groups):
+            raw = held([P, PACK, GROUP], F32, "wa_raw%d" % g)
+            nc.sync.dma_start(out=raw[:], in_=wa_rows[:, :, g * GROUP : (g + 1) * GROUP])
+            wa_raw.append(raw)
+        pos1_sb = held([P, M // 16], U16, "pos1_sb")
+        nc.sync.dma_start(pos1_sb[:], pos1)
+        pos2_sb = held([P, M // 16], U16, "pos2_sb")
+        nc.sync.dma_start(pos2_sb[:], pos2)
+        temp_sb = held([P, groups, PACK], F32, "temp_sb")
+        nc.sync.dma_start(out=temp_sb[:], in_=temp.rearrange("(g p t) -> p g t", p=P, t=PACK))
+        gain_sb = held([P, groups, PACK], F32, "gain_sb")
+        nc.sync.dma_start(out=gain_sb[:], in_=gain.rearrange("(g p t) -> p g t", p=P, t=PACK))
+        signs_sb = []
+        for g in range(groups):
+            rows = held([P, PACK, M], F32, "signs%d" % g)
+            nc.sync.dma_start(out=rows[:], in_=signs[g * GROUP : (g + 1) * GROUP, :].rearrange("(p t) m -> p t m", t=PACK))
+            signs_sb.append(rows)
+
+        v_scales = held([P, passes, S], U8, "v_scales")
+        v_words = held([P, passes, S], U32, "v_words")
+        for a in range(passes):
+            nc.vector.tensor_copy(v_scales[:, a, :], scale_win[:, a, :].indirect(offs_sb[:]))
+        nc.vector.tensor_copy(v_words[:, 0, :], word_win[0][:].indirect(offs_sb[:]))
+        for u in range(halves):
+            nc.vector.tensor_copy(
+                v_words[:, 1, u * BANK : (u + 1) * BANK],
+                word_win[1][:].indirect(offs_sb[:, u * BANK // 16 : (u + 1) * BANK // 16]),
+            )
+
+        w2_codes = held([P, passes, 2 * H], U8, "w2_codes")
+        nc.scalar.copy(
+            out=w2_codes[:].bitcast(U16).rearrange("p a (t m) -> p a m t", t=PACK),
+            in_=w2w_raw[:].bitcast(U16).rearrange("p a (m t) -> p a m t", t=PACK),
+        )
+        w2_plane = held([P, passes, H], U8, "w2_plane")
+        nc.vector.tensor_copy(
+            out=w2_plane[:].rearrange("p a (t m) -> p a m t", t=PACK),
+            in_=w2s_raw[:].rearrange("p a (m t) -> p a m t", t=PACK),
+        )
+
+        def round_weights(raw):
+            rounded = ring.tile([P, PACK * GROUP], BF16, name="w_rounded", align_bytes=64, bufs=2)
+            nc.scalar.copy(
+                out=rounded[:].rearrange("p (t m i) -> p m i t", t=PACK, i=PACK),
+                in_=raw[:].rearrange("p i (m t) -> p m i t", t=PACK),
+            )
+            return rounded
+
+        def quantize(rounded, name):
+            codes = held([P, GROUP], U32, name + "_codes")
+            plane = held([P, GROUP], U8, name + "_plane")
+            nc.vector.quantize_mx(out=codes[:].bitcast(FP8X4), scales=plane[:], in_=rounded[:])
+            return codes, plane
+
+        w1_mx = [quantize(round_weights(w1_raw[a]), "w1_%d" % a) for a in range(passes)]
+
+        neg_temp = held([P, groups, PACK], F32, "neg_temp")
+        nc.gpsimd.tensor_scalar(neg_temp[:], temp_sb[:], -1.0, 0.0, ALU.mult, ALU.add)
+
+        modulated = held([P, PACK, S], F32, "modulated")
+        for t in range(PACK):
+            for u in range(halves):
+                cols = slice(u * BANK, (u + 1) * BANK)
+                acc = psum.tile([P, BANK], F32, name="bank")
+                for a in range(passes):
+                    nc.tensor.matmul_mx(
+                        out=acc[:],
+                        lhsT=w2_codes[:, a, 2 * P * t : 2 * P * (t + 1)].bitcast(FP4X4),
+                        lhsT_scale=w2_plane[:, a, P * t : P * (t + 1)],
+                        rhs=v_words[:, a, cols].bitcast(FP8X4),
+                        rhs_scale=v_scales[:, a, cols],
+                        start=(a == 0),
+                        stop=(a == passes - 1),
+                    )
+                nc.vector.tensor_tensor(modulated[:, t, cols], acc[:], motion_sb[t][:, cols], ALU.mult)
+
+        wa_rounded = [round_weights(wa_raw[g]) for g in range(groups)]
+        wa_mx = []
+        h_mx = []
+        for u in range(halves):
+            h_rounded = ring.tile([P, PACK * BANK], BF16, name="h_rounded", align_bytes=64, bufs=2)
+            for b in range(BANK // P):
+                cols = slice(u * BANK + b * P, u * BANK + (b + 1) * P)
+                acc = psum.tile([P, PACK, P], F32, name="bank")
+                for t in range(PACK):
+                    for a in range(passes):
+                        codes, plane = w1_mx[a]
+                        nc.tensor.matmul_mx(
+                            out=acc[:, t, :],
+                            lhsT=codes[:, P * t : P * (t + 1)].bitcast(FP8X4),
+                            lhsT_scale=plane[:, P * t : P * (t + 1)],
+                            rhs=v_words[:, a, cols].bitcast(FP8X4),
+                            rhs_scale=v_scales[:, a, cols],
+                            start=(a == 0),
+                            stop=(a == passes - 1),
+                        )
+                nc.vector.tensor_tensor(
+                    h_rounded[:, b * GROUP : (b + 1) * GROUP].rearrange("p (c i t) -> p c t i", i=4, t=PACK),
+                    acc[:].rearrange("p t (c i) -> p c t i", i=4),
+                    modulated[:, :, cols].rearrange("p t (c i) -> p c t i", i=4),
+                    ALU.add,
+                )
+                if b == 0:
+                    wa_mx.append(quantize(wa_rounded[u], "wa_%d" % u))
+            h_mx.append(quantize(h_rounded, "h_%d" % u))
+
+        tiles = groups * PACK
+        top_half = held([P, tiles], F32, "top_half")
+        top = held([P, tiles], F32, "top")
+        bias = held([P, tiles], F32, "bias")
+        temp_col = temp_sb[:].rearrange("p g t -> p (g t)")
+        neg_temp_col = neg_temp[:].rearrange("p g t -> p (g t)")
+        gain_col = gain_sb[:].rearrange("p g t -> p (g t)")
+        y = [held([P, PACK, M], F32, "y%d" % g) for g in range(groups)]
+        y_plane = held([P, groups, M], U8, "y_plane")
+        e_tiles, looks, picks, signed = {}, {}, {}, {}
+
+        def scores(i, u):
+            g, t = divmod(i, PACK)
+            if u == 0:
+                e_tiles[i] = ring.tile([P, S], F32, name="e", bufs=3)
+            acc = psum.tile([P, BANK], F32, name="bank")
+            nc.tensor.matmul_mx(
+                out=acc[:],
+                lhsT=wa_mx[g][0][:, P * t : P * (t + 1)].bitcast(FP8X4),
+                lhsT_scale=wa_mx[g][1][:, P * t : P * (t + 1)],
+                rhs=h_mx[u][0][:].bitcast(FP8X4),
+                rhs_scale=h_mx[u][1][:],
+                start=True,
+                stop=True,
+            )
+            nc.vector.tensor_scalar(
+                e_tiles[i][:, u * BANK : (u + 1) * BANK], acc[:], 1.0,
+                None if u == 0 else top_half[:, i : i + 1], ALU.mult, ALU.max,
+                accum_out=(top_half if u == 0 else top)[:, i : i + 1],
+            )
+
+        def look(i):
+            nc.scalar.activation(bias[:, i : i + 1], top[:, i : i + 1], ACT.Copy, scale=neg_temp_col[:, i : i + 1])
+            looks[i] = ring.tile([P, M], F32, name="look")
+            nc.scalar.activation(
+                looks[i][:], e_tiles[i][:].indirect(pos1_sb[:]), ACT.Exp,
+                bias=bias[:, i : i + 1], scale=temp_col[:, i : i + 1],
+            )
+
+        def pick(i):
+            picks[i] = ring.tile([P, M], F32, name="pick")
+            nc.vector.tensor_copy(picks[i][:], e_tiles[i][:].indirect(pos2_sb[:]))
+
+        def sign(i):
+            g, t = divmod(i, PACK)
+            signed[i] = ring.tile([P, M], F32, name="signed")
+            nc.vector.scalar_tensor_tensor(
+                signed[i][:], looks[i][:], gain_col[:, i : i + 1], signs_sb[g][:, t, :], ALU.mult, ALU.mult
+            )
+
+        def cap(i):
+            g, t = divmod(i, PACK)
+            nc.vector.scalar_tensor_tensor(
+                y[g][:, t, :], picks[i][:], gain_col[:, i : i + 1], signed[i][:], ALU.mult, ALU.min
+            )
+            rows = out_0[g * GROUP : (g + 1) * GROUP, :].rearrange("(p t) m -> p t m", t=PACK)
+            nc.sync.dma_start(out=rows[:, t, :], in_=y[g][:, t, :])
+
+        rounded_y = {}
+
+        def round_page(g):
+            rounded_y[g] = ring.tile([P, PACK * M], BF16, name="y_rounded", align_bytes=64, bufs=2)
+            nc.scalar.copy(
+                out=rounded_y[g][:].rearrange("p (c i t) -> p c t i", i=4, t=PACK),
+                in_=y[g][:].rearrange("p t (c i) -> p c t i", i=4),
+            )
+
+        def quantize_page(g):
+            codes = held([P, M], U32, "y_codes%d" % g)
+            nc.vector.quantize_mx(out=codes[:].bitcast(FP8X4), scales=y_plane[:, g, :], in_=rounded_y[g][:])
+            nc.sync.dma_start(out=out_1[g].rearrange("p m t -> p (m t)").bitcast(I32), in_=codes[:].bitcast(I32))
+
+        for i in range(tiles + 1):
+            if i < tiles:
+                scores(i, 0)
+            if i > 0:
+                sign(i - 1)
+            if i < tiles:
+                scores(i, 1)
+                look(i)
+            if i > 0:
+                cap(i - 1)
+            if i < tiles:
+                pick(i)
+            if i > 0 and i % PACK == 0:
+                round_page(i // PACK - 1)
+            if i == PACK + 2:
+                quantize_page(0)
+        quantize_page(groups - 1)
+        for q in range(QUADS):
+            queue = nc.sync if q % 2 == 0 else nc.scalar
+            queue.dma_start(
+                out=out_2[:, 4 * q : 4 * q + 4, :].rearrange("g r m -> r g m").bitcast(I32),
+                in_=y_plane[32 * q : 32 * q + 4, :, :].bitcast(I32),
+            )

@@ -45,42 +45,19 @@ def tile_list_stream_membership_page_kernel(
         w2s_raw = held([P, passes, H], U8, "w2s_raw")
         nc.gpsimd.memset(w2s_raw[:].bitcast(I32), 0)
 
+        def shared(shape, dtype, name, tag):
+            return keep.tile(shape, dtype, name=name, tag=tag, align_bytes=64)
+
         offs_sb = held([P, S // 16], U16, "offs_sb")
         nc.sync.dma_start(offs_sb[:], offs)
-        for q in range(QUADS):
-            nc.scalar.dma_start(
-                out=scale_win[32 * q : 32 * q + 4, :, :].bitcast(I32),
-                in_=tab_scales[:, 4 * q : 4 * q + 4, :].rearrange("a r t -> r a t").bitcast(I32),
+        word_win = [shared([P, T], U32, "word_win%d" % a, "early%d" % a) for a in range(passes)]
+
+        def load_words(a):
+            nc.sync.dma_start(
+                out=word_win[a][:].bitcast(I32), in_=tab_words[a].rearrange("p t i -> p (t i)").bitcast(I32)
             )
-        word_win = []
-        for a in range(passes):
-            win = held([P, T], U32, "word_win%d" % a)
-            nc.sync.dma_start(out=win[:].bitcast(I32), in_=tab_words[a].rearrange("p t i -> p (t i)").bitcast(I32))
-            word_win.append(win)
-        w2w_raw = held([P, passes, 2 * H], U8, "w2w_raw")
-        nc.sync.dma_start(out=w2w_raw[:].bitcast(I32), in_=w2_words.rearrange("a p b -> p a b").bitcast(I32))
-        for q in range(QUADS):
-            nc.scalar.dma_start(
-                out=w2s_raw[32 * q : 32 * q + 4, :, :].bitcast(I32),
-                in_=w2_scales[:, 4 * q : 4 * q + 4, :].rearrange("a r c -> r a c").bitcast(I32),
-            )
-        w1_raw = []
-        for a in range(passes):
-            raw = held([P, PACK, H], F32, "w1_raw%d" % a)
-            nc.sync.dma_start(out=raw[:], in_=w1[a * GROUP : (a + 1) * GROUP, :].rearrange("(p i) c -> p i c", i=PACK))
-            w1_raw.append(raw)
-        motion_rows = motion.rearrange("(p t) j -> p t j", t=PACK)
-        motion_sb = []
-        for t in range(PACK):
-            rows = held([P, S], F32, "motion%d" % t)
-            nc.sync.dma_start(out=rows[:], in_=motion_rows[:, t, :])
-            motion_sb.append(rows)
-        wa_rows = wa.rearrange("(p i) n -> p i n", i=PACK)
-        wa_raw = []
-        for g in range(groups):
-            raw = held([P, PACK, GROUP], F32, "wa_raw%d" % g)
-            nc.sync.dma_start(out=raw[:], in_=wa_rows[:, :, g * GROUP : (g + 1) * GROUP])
-            wa_raw.append(raw)
+
+        load_words(0)
         pos1_sb = held([P, M // 16], U16, "pos1_sb")
         nc.sync.dma_start(pos1_sb[:], pos1)
         pos2_sb = held([P, M // 16], U16, "pos2_sb")
@@ -89,22 +66,35 @@ def tile_list_stream_membership_page_kernel(
         nc.sync.dma_start(out=temp_sb[:], in_=temp.rearrange("(g p t) -> p g t", p=P, t=PACK))
         gain_sb = held([P, groups, PACK], F32, "gain_sb")
         nc.sync.dma_start(out=gain_sb[:], in_=gain.rearrange("(g p t) -> p g t", p=P, t=PACK))
-        signs_sb = []
-        for g in range(groups):
-            rows = held([P, PACK, M], F32, "signs%d" % g)
-            nc.sync.dma_start(out=rows[:], in_=signs[g * GROUP : (g + 1) * GROUP, :].rearrange("(p t) m -> p t m", t=PACK))
-            signs_sb.append(rows)
+        load_words(1)
+        w2w_raw = held([P, passes, 2 * H], U8, "w2w_raw")
+        nc.sync.dma_start(out=w2w_raw[:].bitcast(I32), in_=w2_words.rearrange("a p b -> p a b").bitcast(I32))
+        for q in range(QUADS):
+            nc.scalar.dma_start(
+                out=scale_win[32 * q : 32 * q + 4, :, :].bitcast(I32),
+                in_=tab_scales[:, 4 * q : 4 * q + 4, :].rearrange("a r t -> r a t").bitcast(I32),
+            )
+        for q in range(QUADS):
+            nc.scalar.dma_start(
+                out=w2s_raw[32 * q : 32 * q + 4, :, :].bitcast(I32),
+                in_=w2_scales[:, 4 * q : 4 * q + 4, :].rearrange("a r c -> r a c").bitcast(I32),
+            )
+        w1_raw = []
+        for a in range(passes):
+            raw = shared([P, PACK, H], F32, "w1_raw%d" % a, "weights%d" % a)
+            nc.sync.dma_start(out=raw[:], in_=w1[a * GROUP : (a + 1) * GROUP, :].rearrange("(p i) c -> p i c", i=PACK))
+            w1_raw.append(raw)
 
         v_scales = held([P, passes, S], U8, "v_scales")
         v_words = held([P, passes, S], U32, "v_words")
         for a in range(passes):
-            nc.vector.tensor_copy(v_scales[:, a, :], scale_win[:, a, :].indirect(offs_sb[:]))
-        nc.vector.tensor_copy(v_words[:, 0, :], word_win[0][:].indirect(offs_sb[:]))
-        for u in range(halves):
-            nc.vector.tensor_copy(
-                v_words[:, 1, u * BANK : (u + 1) * BANK],
-                word_win[1][:].indirect(offs_sb[:, u * BANK // 16 : (u + 1) * BANK // 16]),
-            )
+            nc.vector.tensor_copy(v_words[:, a, :], word_win[a][:].indirect(offs_sb[:]))
+        motion_rows = motion.rearrange("(p t) j -> p t j", t=PACK)
+        motion_sb = []
+        for a in range(2):
+            rows = shared([P, 2, S], F32, "motion%d" % a, "early%d" % a)
+            nc.sync.dma_start(out=rows[:], in_=motion_rows[:, 2 * a : 2 * a + 2, :])
+            motion_sb.append(rows)
 
         w2_codes = held([P, passes, 2 * H], U8, "w2_codes")
         nc.scalar.copy(
@@ -116,6 +106,13 @@ def tile_list_stream_membership_page_kernel(
             out=w2_plane[:].rearrange("p a (t m) -> p a m t", t=PACK),
             in_=w2s_raw[:].rearrange("p a (m t) -> p a m t", t=PACK),
         )
+
+        nc.vector.tensor_copy(v_scales[:, 0, :], scale_win[:, 0, :].indirect(offs_sb[:]))
+        for u in range(halves):
+            nc.vector.tensor_copy(
+                v_scales[:, 1, u * BANK : (u + 1) * BANK],
+                scale_win[:, 1, :].indirect(offs_sb[:, u * BANK // 16 : (u + 1) * BANK // 16]),
+            )
 
         def round_weights(raw):
             rounded = ring.tile([P, PACK * GROUP], BF16, name="w_rounded", align_bytes=64, bufs=2)
@@ -132,6 +129,13 @@ def tile_list_stream_membership_page_kernel(
             return codes, plane
 
         w1_mx = [quantize(round_weights(w1_raw[a]), "w1_%d" % a) for a in range(passes)]
+
+        wa_rows = wa.rearrange("(p i) n -> p i n", i=PACK)
+        wa_raw = []
+        for g in range(groups):
+            raw = shared([P, PACK, GROUP], F32, "wa_raw%d" % g, "weights%d" % g)
+            nc.sync.dma_start(out=raw[:], in_=wa_rows[:, :, g * GROUP : (g + 1) * GROUP])
+            wa_raw.append(raw)
 
         neg_temp = held([P, groups, PACK], F32, "neg_temp")
         nc.gpsimd.tensor_scalar(neg_temp[:], temp_sb[:], -1.0, 0.0, ALU.mult, ALU.add)
@@ -151,7 +155,13 @@ def tile_list_stream_membership_page_kernel(
                         start=(a == 0),
                         stop=(a == passes - 1),
                     )
-                nc.vector.tensor_tensor(modulated[:, t, cols], acc[:], motion_sb[t][:, cols], ALU.mult)
+                nc.vector.tensor_tensor(modulated[:, t, cols], acc[:], motion_sb[t // 2][:, t % 2, cols], ALU.mult)
+
+        signs_sb = []
+        for g in range(groups):
+            rows = shared([P, PACK, M], F32, "signs%d" % g, "early%d" % g)
+            nc.sync.dma_start(out=rows[:], in_=signs[g * GROUP : (g + 1) * GROUP, :].rearrange("(p t) m -> p t m", t=PACK))
+            signs_sb.append(rows)
 
         wa_rounded = [round_weights(wa_raw[g]) for g in range(groups)]
         wa_mx = []
@@ -174,9 +184,9 @@ def tile_list_stream_membership_page_kernel(
                             stop=(a == passes - 1),
                         )
                 nc.vector.tensor_tensor(
-                    h_rounded[:, b * GROUP : (b + 1) * GROUP].rearrange("p (c i t) -> p c t i", i=4, t=PACK),
-                    acc[:].rearrange("p t (c i) -> p c t i", i=4),
-                    modulated[:, :, cols].rearrange("p t (c i) -> p c t i", i=4),
+                    h_rounded[:, b * GROUP : (b + 1) * GROUP].rearrange("p (c i t) -> p c t i", i=2, t=PACK),
+                    acc[:].rearrange("p t (c i) -> p c t i", i=2),
+                    modulated[:, :, cols].rearrange("p t (c i) -> p c t i", i=2),
                     ALU.add,
                 )
                 if b == 0:
@@ -192,7 +202,7 @@ def tile_list_stream_membership_page_kernel(
         gain_col = gain_sb[:].rearrange("p g t -> p (g t)")
         y = [held([P, PACK, M], F32, "y%d" % g) for g in range(groups)]
         y_plane = held([P, groups, M], U8, "y_plane")
-        e_tiles, looks, picks, signed = {}, {}, {}, {}
+        e_tiles, looks, picks, signed, weights = {}, {}, {}, {}, {}
 
         def scores(i, u):
             g, t = divmod(i, PACK)
@@ -226,12 +236,14 @@ def tile_list_stream_membership_page_kernel(
             picks[i] = ring.tile([P, M], F32, name="pick")
             nc.vector.tensor_copy(picks[i][:], e_tiles[i][:].indirect(pos2_sb[:]))
 
-        def sign(i):
+        def weigh(i):
             g, t = divmod(i, PACK)
+            weights[i] = ring.tile([P, M], F32, name="weights")
+            nc.scalar.activation(weights[i][:], signs_sb[g][:, t, :], ACT.Copy, scale=gain_col[:, i : i + 1])
+
+        def sign(i):
             signed[i] = ring.tile([P, M], F32, name="signed")
-            nc.vector.scalar_tensor_tensor(
-                signed[i][:], looks[i][:], gain_col[:, i : i + 1], signs_sb[g][:, t, :], ALU.mult, ALU.mult
-            )
+            nc.gpsimd.tensor_tensor(signed[i][:], looks[i][:], weights[i][:], ALU.mult)
 
         def cap(i):
             g, t = divmod(i, PACK)
@@ -246,8 +258,8 @@ def tile_list_stream_membership_page_kernel(
         def round_page(g):
             rounded_y[g] = ring.tile([P, PACK * M], BF16, name="y_rounded", align_bytes=64, bufs=2)
             nc.scalar.copy(
-                out=rounded_y[g][:].rearrange("p (c i t) -> p c t i", i=4, t=PACK),
-                in_=y[g][:].rearrange("p t (c i) -> p c t i", i=4),
+                out=rounded_y[g][:].rearrange("p (c i t) -> p c t i", i=2, t=PACK),
+                in_=y[g][:].rearrange("p t (c i) -> p c t i", i=2),
             )
 
         def quantize_page(g):
@@ -257,12 +269,11 @@ def tile_list_stream_membership_page_kernel(
 
         for i in range(tiles + 1):
             if i < tiles:
+                weigh(i)
                 scores(i, 0)
-            if i > 0:
-                sign(i - 1)
-            if i < tiles:
                 scores(i, 1)
                 look(i)
+                sign(i)
             if i > 0:
                 cap(i - 1)
             if i < tiles:

@@ -40,13 +40,13 @@ def tile_list_stream_membership_page_kernel(
         def held(shape, dtype, name):
             return keep.tile(shape, dtype, name=name, align_bytes=64)
 
-        scale_win = held([P, passes, T], U8, "scale_win")
+        def shared(shape, dtype, name, tag):
+            return keep.tile(shape, dtype, name=name, tag=tag, align_bytes=64)
+
+        scale_win = shared([P, passes, T], U8, "scale_win", "buf_s")
         nc.vector.memset(scale_win[:].bitcast(I32), 0)
         w2s_raw = held([P, passes, H], U8, "w2s_raw")
         nc.gpsimd.memset(w2s_raw[:].bitcast(I32), 0)
-
-        def shared(shape, dtype, name, tag):
-            return keep.tile(shape, dtype, name=name, tag=tag, align_bytes=64)
 
         offs_sb = held([P, S // 16], U16, "offs_sb")
         nc.sync.dma_start(offs_sb[:], offs)
@@ -79,32 +79,46 @@ def tile_list_stream_membership_page_kernel(
                 out=w2s_raw[32 * q : 32 * q + 4, :, :].bitcast(I32),
                 in_=w2_scales[:, 4 * q : 4 * q + 4, :].rearrange("a r c -> r a c").bitcast(I32),
             )
-        w1_raw = []
-        for a in range(passes):
-            raw = shared([P, PACK, H], F32, "w1_raw%d" % a, "weights%d" % a)
+
+        def load_w1(a, tag):
+            raw = shared([P, PACK, H], F32, "w1_raw%d" % a, tag)
             nc.sync.dma_start(out=raw[:], in_=w1[a * GROUP : (a + 1) * GROUP, :].rearrange("(p i) c -> p i c", i=PACK))
-            w1_raw.append(raw)
+            return raw
+
+        def load_motion(a, tag):
+            rows = shared([P, 2, S], F32, "motion%d" % a, tag)
+            nc.sync.dma_start(out=rows[:], in_=motion.rearrange("(p t) j -> p t j", t=PACK)[:, 2 * a : 2 * a + 2, :])
+            return rows
+
+        def load_wa(g, tag):
+            raw = shared([P, PACK, GROUP], F32, "wa_raw%d" % g, tag)
+            nc.sync.dma_start(out=raw[:], in_=wa.rearrange("(p i) n -> p i n", i=PACK)[:, :, g * GROUP : (g + 1) * GROUP])
+            return raw
+
+        def load_signs(g, tag):
+            rows = shared([P, PACK, M], F32, "signs%d" % g, tag)
+            nc.sync.dma_start(out=rows[:], in_=signs[g * GROUP : (g + 1) * GROUP, :].rearrange("(p t) m -> p t m", t=PACK))
+            return rows
+
+        w1_raw0 = load_w1(0, "buf_w")
+        motion_sb = [load_motion(0, "buf_m")]
 
         v_scales = held([P, passes, S], U8, "v_scales")
         v_words = held([P, passes, S], U32, "v_words")
         for a in range(passes):
             nc.vector.tensor_copy(v_words[:, a, :], word_win[a][:].indirect(offs_sb[:]))
-        motion_rows = motion.rearrange("(p t) j -> p t j", t=PACK)
-        motion_sb = []
-        for a in range(2):
-            rows = shared([P, 2, S], F32, "motion%d" % a, "early%d" % a)
-            nc.sync.dma_start(out=rows[:], in_=motion_rows[:, 2 * a : 2 * a + 2, :])
-            motion_sb.append(rows)
+        w1_raw1 = load_w1(1, "early1")
+        motion_sb.append(load_motion(1, "early0"))
 
         w2_codes = held([P, passes, 2 * H], U8, "w2_codes")
         nc.scalar.copy(
-            out=w2_codes[:].bitcast(U16).rearrange("p a (t m) -> p a m t", t=PACK),
-            in_=w2w_raw[:].bitcast(U16).rearrange("p a (m t) -> p a m t", t=PACK),
+            out=w2_codes[:].bitcast(U16).rearrange("p a (t m) -> p a t m", t=PACK),
+            in_=w2w_raw[:].bitcast(U16).rearrange("p a (m t) -> p a t m", t=PACK),
         )
         w2_plane = held([P, passes, H], U8, "w2_plane")
         nc.vector.tensor_copy(
-            out=w2_plane[:].rearrange("p a (t m) -> p a m t", t=PACK),
-            in_=w2s_raw[:].rearrange("p a (m t) -> p a m t", t=PACK),
+            out=w2_plane[:].rearrange("p a (t m) -> p a t m", t=PACK),
+            in_=w2s_raw[:].rearrange("p a (m t) -> p a t m", t=PACK),
         )
 
         nc.vector.tensor_copy(v_scales[:, 0, :], scale_win[:, 0, :].indirect(offs_sb[:]))
@@ -114,11 +128,10 @@ def tile_list_stream_membership_page_kernel(
                 scale_win[:, 1, :].indirect(offs_sb[:, u * BANK // 16 : (u + 1) * BANK // 16]),
             )
 
-        def round_weights(raw):
-            rounded = ring.tile([P, PACK * GROUP], BF16, name="w_rounded", align_bytes=64, bufs=2)
+        def round_weights(raw, rounded):
             nc.scalar.copy(
-                out=rounded[:].rearrange("p (t m i) -> p m i t", t=PACK, i=PACK),
-                in_=raw[:].rearrange("p i (m t) -> p m i t", t=PACK),
+                out=rounded[:].rearrange("p (s t m i) -> p s m i t", s=2, t=2, i=PACK),
+                in_=raw[:].rearrange("p i (m s t) -> p s m i t", s=2, t=2),
             )
             return rounded
 
@@ -128,17 +141,14 @@ def tile_list_stream_membership_page_kernel(
             nc.vector.quantize_mx(out=codes[:].bitcast(FP8X4), scales=plane[:], in_=rounded[:])
             return codes, plane
 
-        w1_mx = [quantize(round_weights(w1_raw[a]), "w1_%d" % a) for a in range(passes)]
-
-        wa_rows = wa.rearrange("(p i) n -> p i n", i=PACK)
-        wa_raw = []
-        for g in range(groups):
-            raw = shared([P, PACK, GROUP], F32, "wa_raw%d" % g, "weights%d" % g)
-            nc.sync.dma_start(out=raw[:], in_=wa_rows[:, :, g * GROUP : (g + 1) * GROUP])
-            wa_raw.append(raw)
-
         neg_temp = held([P, groups, PACK], F32, "neg_temp")
-        nc.gpsimd.tensor_scalar(neg_temp[:], temp_sb[:], -1.0, 0.0, ALU.mult, ALU.add)
+        nc.scalar.activation(neg_temp[:], temp_sb[:], ACT.Identity, scale=-1.0)
+        w1_rounded = [
+            round_weights(raw, shared([P, PACK * GROUP], BF16, "w1_rounded%d" % a, "rounded%d" % a))
+            for a, raw in enumerate((w1_raw0, w1_raw1))
+        ]
+        wa_raw = [load_wa(0, "buf_s"), load_wa(1, "buf_w")]
+        w1_mx = []
 
         modulated = held([P, PACK, S], F32, "modulated")
         for t in range(PACK):
@@ -156,42 +166,55 @@ def tile_list_stream_membership_page_kernel(
                         stop=(a == passes - 1),
                     )
                 nc.vector.tensor_tensor(modulated[:, t, cols], acc[:], motion_sb[t // 2][:, t % 2, cols], ALU.mult)
+            if t in (1, 2):
+                w1_mx.append(quantize(w1_rounded[t - 1], "w1_%d" % (t - 1)))
 
-        signs_sb = []
-        for g in range(groups):
-            rows = shared([P, PACK, M], F32, "signs%d" % g, "early%d" % g)
-            nc.sync.dma_start(out=rows[:], in_=signs[g * GROUP : (g + 1) * GROUP, :].rearrange("(p t) m -> p t m", t=PACK))
-            signs_sb.append(rows)
+        signs_sb = [load_signs(0, "early1"), load_signs(1, "buf_m")]
+        wa_rounded = [round_weights(wa_raw[0], shared([P, PACK * GROUP], BF16, "wa_rounded0", "rounded0"))]
 
-        wa_rounded = [round_weights(wa_raw[g]) for g in range(groups)]
-        wa_mx = []
-        h_mx = []
+        def interleave(rows, first, width, name, copy):
+            grouped = held([P, PACK * width], BF16, name)
+            copy(
+                out=grouped[:].rearrange("p (c i t) -> p c t i", i=4, t=PACK),
+                in_=rows[:, :, first : first + width].rearrange("p t (c i) -> p c t i", i=4),
+            )
+            return grouped
+
+        h_rows = []
         for u in range(halves):
-            h_rounded = ring.tile([P, PACK * BANK], BF16, name="h_rounded", align_bytes=64, bufs=2)
-            for b in range(BANK // P):
-                cols = slice(u * BANK + b * P, u * BANK + (b + 1) * P)
-                acc = psum.tile([P, PACK, P], F32, name="bank")
-                for t in range(PACK):
-                    for a in range(passes):
-                        codes, plane = w1_mx[a]
-                        nc.tensor.matmul_mx(
-                            out=acc[:, t, :],
-                            lhsT=codes[:, P * t : P * (t + 1)].bitcast(FP8X4),
-                            lhsT_scale=plane[:, P * t : P * (t + 1)],
-                            rhs=v_words[:, a, cols].bitcast(FP8X4),
-                            rhs_scale=v_scales[:, a, cols],
-                            start=(a == 0),
-                            stop=(a == passes - 1),
-                        )
-                nc.vector.tensor_tensor(
-                    h_rounded[:, b * GROUP : (b + 1) * GROUP].rearrange("p (c i t) -> p c t i", i=2, t=PACK),
-                    acc[:].rearrange("p t (c i) -> p c t i", i=2),
-                    modulated[:, :, cols].rearrange("p t (c i) -> p c t i", i=2),
-                    ALU.add,
-                )
-                if b == 0:
-                    wa_mx.append(quantize(wa_rounded[u], "wa_%d" % u))
-            h_mx.append(quantize(h_rounded, "h_%d" % u))
+            cols = slice(u * BANK, (u + 1) * BANK)
+            rows = shared([P, PACK, BANK], BF16, "h_rows%d" % u, "h_rows%d" % u)
+            for t in range(PACK):
+                acc = psum.tile([P, BANK], F32, name="bank")
+                for a in range(passes):
+                    codes, plane = w1_mx[a]
+                    nc.tensor.matmul_mx(
+                        out=acc[:],
+                        lhsT=codes[:, P * t : P * (t + 1)].bitcast(FP8X4),
+                        lhsT_scale=plane[:, P * t : P * (t + 1)],
+                        rhs=v_words[:, a, cols].bitcast(FP8X4),
+                        rhs_scale=v_scales[:, a, cols],
+                        start=(a == 0),
+                        stop=(a == passes - 1),
+                    )
+                nc.vector.tensor_tensor(rows[:, t, :], acc[:], modulated[:, t, cols], ALU.add)
+            h_rows.append(rows)
+            if u == 0:
+                h_first = interleave(rows, 0, BANK, "h_first", nc.scalar.copy)
+        wa_mx = [quantize(wa_rounded[0], "wa_0")]
+        h_left = interleave(h_rows[1], 0, BANK // 2, "h_left", nc.vector.tensor_copy)
+        h_right = interleave(h_rows[1], BANK // 2, BANK // 2, "h_right", nc.scalar.copy)
+        wa_rounded.append(round_weights(wa_raw[1], shared([P, PACK * GROUP], BF16, "wa_rounded1", "h_rows0")))
+        h_mx = [quantize(h_first, "h_0")]
+        h_codes = held([P, BANK], U32, "h_1_codes")
+        h_plane = held([P, BANK], U8, "h_1_plane")
+        h_mx.append((h_codes, h_plane))
+
+        def quantize_h(grouped, first):
+            cols = slice(first, first + BANK // 2)
+            nc.vector.quantize_mx(out=h_codes[:, cols].bitcast(FP8X4), scales=h_plane[:, cols], in_=grouped[:])
+
+        quantize_h(h_left, 0)
 
         tiles = groups * PACK
         top_half = held([P, tiles], F32, "top_half")
@@ -233,7 +256,7 @@ def tile_list_stream_membership_page_kernel(
             )
 
         def pick(i):
-            picks[i] = ring.tile([P, M], F32, name="pick")
+            picks[i] = ring.tile([P, M], F32, name="pick", bufs=4)
             nc.vector.tensor_copy(picks[i][:], e_tiles[i][:].indirect(pos2_sb[:]))
 
         def weigh(i):
@@ -243,46 +266,70 @@ def tile_list_stream_membership_page_kernel(
 
         def sign(i):
             signed[i] = ring.tile([P, M], F32, name="signed")
-            nc.gpsimd.tensor_tensor(signed[i][:], looks[i][:], weights[i][:], ALU.mult)
+            engine = nc.vector if i == tiles - 1 else nc.gpsimd
+            engine.tensor_tensor(signed[i][:], looks[i][:], weights[i][:], ALU.mult)
 
-        def cap(i):
+        def cap(i, cols):
             g, t = divmod(i, PACK)
             nc.vector.scalar_tensor_tensor(
-                y[g][:, t, :], picks[i][:], gain_col[:, i : i + 1], signed[i][:], ALU.mult, ALU.min
+                y[g][:, t, cols], picks[i][:, cols], gain_col[:, i : i + 1], signed[i][:, cols], ALU.mult, ALU.min
             )
+
+        def store_rows(i):
+            g, t = divmod(i, PACK)
             rows = out_0[g * GROUP : (g + 1) * GROUP, :].rearrange("(p t) m -> p t m", t=PACK)
             nc.sync.dma_start(out=rows[:, t, :], in_=y[g][:, t, :])
 
-        rounded_y = {}
-
-        def round_page(g):
-            rounded_y[g] = ring.tile([P, PACK * M], BF16, name="y_rounded", align_bytes=64, bufs=2)
-            nc.scalar.copy(
-                out=rounded_y[g][:].rearrange("p (c i t) -> p c t i", i=2, t=PACK),
-                in_=y[g][:].rearrange("p t (c i) -> p c t i", i=2),
+        def round_page(g, cols, rounded, first, copy):
+            copy(
+                out=rounded[:, PACK * (cols.start - first) : PACK * (cols.stop - first)].rearrange(
+                    "p (c i t) -> p c t i", i=4, t=PACK
+                ),
+                in_=y[g][:, :, cols].rearrange("p t (c i) -> p c t i", i=4),
             )
 
-        def quantize_page(g):
-            codes = held([P, M], U32, "y_codes%d" % g)
-            nc.vector.quantize_mx(out=codes[:].bitcast(FP8X4), scales=y_plane[:, g, :], in_=rounded_y[g][:])
-            nc.sync.dma_start(out=out_1[g].rearrange("p m t -> p (m t)").bitcast(I32), in_=codes[:].bitcast(I32))
+        def quantize_page(g, cols, rounded):
+            width = cols.stop - cols.start
+            codes = held([P, width], U32, "y_codes%d_%d" % (g, cols.start))
+            nc.vector.quantize_mx(out=codes[:].bitcast(FP8X4), scales=y_plane[:, g, cols], in_=rounded[:])
+            nc.sync.dma_start(
+                out=out_1[g].rearrange("p m t -> p (m t)").bitcast(I32)[:, cols], in_=codes[:].bitcast(I32)
+            )
 
-        for i in range(tiles + 1):
-            if i < tiles:
-                weigh(i)
-                scores(i, 0)
-                scores(i, 1)
-                look(i)
+        whole, left, right = slice(0, M), slice(0, M // 2), slice(M // 2, M)
+        last = tiles - 1
+        first_page = held([P, PACK * M], BF16, "first_page")
+        left_page = held([P, PACK * M // 2], BF16, "left_page")
+        right_page = held([P, PACK * M // 2], BF16, "right_page")
+        scores(0, 0)
+        quantize_h(h_right, BANK // 2)
+        weigh(0)
+        for i in range(tiles):
+            scores(i, 1)
+            look(i)
+            if i < last:
                 sign(i)
-            if i > 0:
-                cap(i - 1)
-            if i < tiles:
-                pick(i)
-            if i > 0 and i % PACK == 0:
-                round_page(i // PACK - 1)
-            if i == PACK + 2:
-                quantize_page(0)
-        quantize_page(groups - 1)
+                weigh(i + 1)
+                scores(i + 1, 0)
+            if i > 1:
+                cap(i - 2, whole)
+                store_rows(i - 2)
+            if i == 1:
+                wa_mx.append(quantize(wa_rounded[1], "wa_1"))
+            pick(i)
+            if i in (PACK + 1, PACK + 2):
+                round_page(0, left if i == PACK + 1 else right, first_page, 0, nc.scalar.copy)
+        cap(last - 1, whole)
+        store_rows(last - 1)
+        quantize_page(0, whole, first_page)
+        sign(last)
+        cap(last, left)
+        round_page(1, left, left_page, left.start, nc.scalar.copy)
+        cap(last, right)
+        store_rows(last)
+        round_page(1, right, right_page, right.start, nc.vector.tensor_copy)
+        quantize_page(1, right, right_page)
+        quantize_page(1, left, left_page)
         for q in range(QUADS):
             queue = nc.sync if q % 2 == 0 else nc.scalar
             queue.dma_start(

from contextlib import ExitStack

import concourse.mybir as mybir

K, H, N, T, S, M = 1024, 512, 1024, 2048, 1024, 512
FLOPS = 2 * (2 * K * H * S + H * N * S)

F32 = mybir.dt.float32
BF16 = mybir.dt.bfloat16
I32 = mybir.dt.int32
U32 = mybir.dt.uint32
U16 = mybir.dt.uint16
U8 = mybir.dt.uint8
FP8X4 = mybir.dt.float8_e4m3fn_x4
FP4X4 = mybir.dt.float4_e2m1fn_x4
ALU = mybir.AluOpType
ACT = mybir.ActivationFunctionType

P = 128
PACK = 4
GROUP = P * PACK
BANK = 512
QUADS = 4


def tile_list_stream_membership_page_kernel(
    tc, tab_words, tab_scales, offs, pos1, pos2, w1, w2_words, w2_scales, motion, wa, temp, signs, gain,
    out_0, out_1, out_2,
):
    nc = tc.nc
    passes = K // GROUP
    groups = N // GROUP
    halves = S // BANK

    with ExitStack() as ctx:
        keep = ctx.enter_context(tc.tile_pool(name="keep", bufs=1))
        ring = ctx.enter_context(tc.tile_pool(name="ring", bufs=3))
        psum = ctx.enter_context(tc.psum_pool(name="psum", bufs=8))

        def held(shape, dtype, name):
            return keep.tile(shape, dtype, name=name, align_bytes=64)

        def shared(shape, dtype, name, tag):
            return keep.tile(shape, dtype, name=name, tag=tag, align_bytes=64)

        scale_win = shared([P, passes, T], U8, "scale_win", "buf_s")
        nc.vector.memset(scale_win[:].bitcast(I32), 0)
        w2s_raw = held([P, passes, H], U8, "w2s_raw")
        nc.gpsimd.memset(w2s_raw[:].bitcast(I32), 0)

        offs_sb = held([P, S // 16], U16, "offs_sb")
        nc.sync.dma_start(offs_sb[:], offs)
        word_win = [shared([P, T], U32, "word_win%d" % a, "early%d" % a) for a in range(passes)]

        def load_words(a):
            nc.sync.dma_start(
                out=word_win[a][:].bitcast(I32), in_=tab_words[a].rearrange("p t i -> p (t i)").bitcast(I32)
            )

        load_words(0)
        pos1_sb = held([P, M // 16], U16, "pos1_sb")
        nc.sync.dma_start(pos1_sb[:], pos1)
        pos2_sb = held([P, M // 16], U16, "pos2_sb")
        nc.sync.dma_start(pos2_sb[:], pos2)
        temp_sb = held([P, groups, PACK], F32, "temp_sb")
        nc.sync.dma_start(out=temp_sb[:], in_=temp.rearrange("(g p t) -> p g t", p=P, t=PACK))
        gain_sb = held([P, groups, PACK], F32, "gain_sb")
        nc.sync.dma_start(out=gain_sb[:], in_=gain.rearrange("(g p t) -> p g t", p=P, t=PACK))
        load_words(1)
        w2w_raw = held([P, passes, 2 * H], U8, "w2w_raw")
        nc.sync.dma_start(out=w2w_raw[:].bitcast(I32), in_=w2_words.rearrange("a p b -> p a b").bitcast(I32))
        for q in range(QUADS):
            nc.scalar.dma_start(
                out=scale_win[32 * q : 32 * q + 4, :, :].bitcast(I32),
                in_=tab_scales[:, 4 * q : 4 * q + 4, :].rearrange("a r t -> r a t").bitcast(I32),
            )
        for q in range(QUADS):
            nc.scalar.dma_start(
                out=w2s_raw[32 * q : 32 * q + 4, :, :].bitcast(I32),
                in_=w2_scales[:, 4 * q : 4 * q + 4, :].rearrange("a r c -> r a c").bitcast(I32),
            )

        def load_w1(a, tag):
            raw = shared([P, PACK, H], F32, "w1_raw%d" % a, tag)
            nc.sync.dma_start(out=raw[:], in_=w1[a * GROUP : (a + 1) * GROUP, :].rearrange("(p i) c -> p i c", i=PACK))
            return raw

        def load_motion(a, tag):
            rows = shared([P, 2, S], F32, "motion%d" % a, tag)
            nc.sync.dma_start(out=rows[:], in_=motion.rearrange("(p t) j -> p t j", t=PACK)[:, 2 * a : 2 * a + 2, :])
            return rows

        def load_wa(g, tag):
            raw = shared([P, PACK, GROUP], F32, "wa_raw%d" % g, tag)
            nc.sync.dma_start(out=raw[:], in_=wa.rearrange("(p i) n -> p i n", i=PACK)[:, :, g * GROUP : (g + 1) * GROUP])
            return raw

        def load_signs(g, tag):
            rows = shared([P, PACK, M], F32, "signs%d" % g, tag)
            nc.sync.dma_start(out=rows[:], in_=signs[g * GROUP : (g + 1) * GROUP, :].rearrange("(p t) m -> p t m", t=PACK))
            return rows

        w1_raw0 = load_w1(0, "buf_w")
        motion_sb = [load_motion(0, "buf_m")]

        v_scales = held([P, passes, S], U8, "v_scales")
        v_words = held([P, passes, S], U32, "v_words")
        for a in range(passes):
            nc.vector.tensor_copy(v_words[:, a, :], word_win[a][:].indirect(offs_sb[:]))
        w1_raw1 = load_w1(1, "early1")
        motion_sb.append(load_motion(1, "early0"))

        w2_codes = held([P, passes, 2 * H], U8, "w2_codes")
        nc.scalar.copy(
            out=w2_codes[:].bitcast(U16).rearrange("p a (t m) -> p a t m", t=PACK),
            in_=w2w_raw[:].bitcast(U16).rearrange("p a (m t) -> p a t m", t=PACK),
        )
        w2_plane = held([P, passes, H], U8, "w2_plane")
        nc.vector.tensor_copy(
            out=w2_plane[:].rearrange("p a (t m) -> p a t m", t=PACK),
            in_=w2s_raw[:].rearrange("p a (m t) -> p a t m", t=PACK),
        )

        nc.vector.tensor_copy(v_scales[:, 0, :], scale_win[:, 0, :].indirect(offs_sb[:]))
        for u in range(halves):
            nc.vector.tensor_copy(
                v_scales[:, 1, u * BANK : (u + 1) * BANK],
                scale_win[:, 1, :].indirect(offs_sb[:, u * BANK // 16 : (u + 1) * BANK // 16]),
            )

        def round_weights(raw, rounded):
            nc.scalar.copy(
                out=rounded[:].rearrange("p (s t m i) -> p s m i t", s=2, t=2, i=PACK),
                in_=raw[:].rearrange("p i (m s t) -> p s m i t", s=2, t=2),
            )
            return rounded

        def quantize(rounded, name):
            codes = held([P, GROUP], U32, name + "_codes")
            plane = held([P, GROUP], U8, name + "_plane")
            nc.vector.quantize_mx(out=codes[:].bitcast(FP8X4), scales=plane[:], in_=rounded[:])
            return codes, plane

        neg_temp = held([P, groups, PACK], F32, "neg_temp")
        nc.scalar.activation(neg_temp[:], temp_sb[:], ACT.Identity, scale=-1.0)
        w1_rounded = [
            round_weights(raw, shared([P, PACK * GROUP], BF16, "w1_rounded%d" % a, "rounded%d" % a))
            for a, raw in enumerate((w1_raw0, w1_raw1))
        ]
        wa_raw = [load_wa(0, "buf_s"), load_wa(1, "buf_w")]
        w1_mx = []

        modulated = held([P, PACK, S], F32, "modulated")
        for t in range(PACK):
            for u in range(halves):
                cols = slice(u * BANK, (u + 1) * BANK)
                acc = psum.tile([P, BANK], F32, name="bank")
                for a in range(passes):
                    nc.tensor.matmul_mx(
                        out=acc[:],
                        lhsT=w2_codes[:, a, 2 * P * t : 2 * P * (t + 1)].bitcast(FP4X4),
                        lhsT_scale=w2_plane[:, a, P * t : P * (t + 1)],
                        rhs=v_words[:, a, cols].bitcast(FP8X4),
                        rhs_scale=v_scales[:, a, cols],
                        start=(a == 0),
                        stop=(a == passes - 1),
                    )
                nc.vector.tensor_tensor(modulated[:, t, cols], acc[:], motion_sb[t // 2][:, t % 2, cols], ALU.mult)
            if t in (1, 2):
                w1_mx.append(quantize(w1_rounded[t - 1], "w1_%d" % (t - 1)))

        signs_sb = [load_signs(0, "early1"), load_signs(1, "buf_m")]
        wa_rounded = [round_weights(wa_raw[0], shared([P, PACK * GROUP], BF16, "wa_rounded0", "rounded0"))]

        def interleave(rows, first, width, name, copy):
            grouped = held([P, PACK * width], BF16, name)
            copy(
                out=grouped[:].rearrange("p (c i t) -> p c t i", i=4, t=PACK),
                in_=rows[:, :, first : first + width].rearrange("p t (c i) -> p c t i", i=4),
            )
            return grouped

        h_rows = []
        for u in range(halves):
            cols = slice(u * BANK, (u + 1) * BANK)
            rows = shared([P, PACK, BANK], BF16, "h_rows%d" % u, "h_rows%d" % u)
            for t in range(PACK):
                acc = psum.tile([P, BANK], F32, name="bank")
                for a in range(passes):
                    codes, plane = w1_mx[a]
                    nc.tensor.matmul_mx(
                        out=acc[:],
                        lhsT=codes[:, P * t : P * (t + 1)].bitcast(FP8X4),
                        lhsT_scale=plane[:, P * t : P * (t + 1)],
                        rhs=v_words[:, a, cols].bitcast(FP8X4),
                        rhs_scale=v_scales[:, a, cols],
                        start=(a == 0),
                        stop=(a == passes - 1),
                    )
                nc.vector.tensor_tensor(rows[:, t, :], acc[:], modulated[:, t, cols], ALU.add)
            h_rows.append(rows)
            if u == 0:
                h_first = interleave(rows, 0, BANK, "h_first", nc.scalar.copy)
        wa_mx = [quantize(wa_rounded[0], "wa_0")]
        h_left = interleave(h_rows[1], 0, BANK // 2, "h_left", nc.vector.tensor_copy)
        h_right = interleave(h_rows[1], BANK // 2, BANK // 2, "h_right", nc.scalar.copy)
        wa_rounded.append(round_weights(wa_raw[1], shared([P, PACK * GROUP], BF16, "wa_rounded1", "h_rows0")))
        h_mx = [quantize(h_first, "h_0")]
        h_codes = held([P, BANK], U32, "h_1_codes")
        h_plane = held([P, BANK], U8, "h_1_plane")
        h_mx.append((h_codes, h_plane))

        def quantize_h(grouped, first):
            cols = slice(first, first + BANK // 2)
            nc.vector.quantize_mx(out=h_codes[:, cols].bitcast(FP8X4), scales=h_plane[:, cols], in_=grouped[:])

        quantize_h(h_left, 0)

        tiles = groups * PACK
        top_half = held([P, tiles], F32, "top_half")
        top = held([P, tiles], F32, "top")
        bias = held([P, tiles], F32, "bias")
        temp_col = temp_sb[:].rearrange("p g t -> p (g t)")
        neg_temp_col = neg_temp[:].rearrange("p g t -> p (g t)")
        gain_col = gain_sb[:].rearrange("p g t -> p (g t)")
        y = [held([P, PACK, M], F32, "y%d" % g) for g in range(groups)]
        y_plane = held([P, groups, M], U8, "y_plane")
        e_tiles, looks, picks, signed, weights = {}, {}, {}, {}, {}

        def scores(i, u):
            g, t = divmod(i, PACK)
            if u == 0:
                e_tiles[i] = ring.tile([P, S], F32, name="e", bufs=3)
            acc = psum.tile([P, BANK], F32, name="bank")
            nc.tensor.matmul_mx(
                out=acc[:],
                lhsT=wa_mx[g][0][:, P * t : P * (t + 1)].bitcast(FP8X4),
                lhsT_scale=wa_mx[g][1][:, P * t : P * (t + 1)],
                rhs=h_mx[u][0][:].bitcast(FP8X4),
                rhs_scale=h_mx[u][1][:],
                start=True,
                stop=True,
            )
            nc.vector.tensor_scalar(
                e_tiles[i][:, u * BANK : (u + 1) * BANK], acc[:], 1.0,
                None if u == 0 else top_half[:, i : i + 1], ALU.mult, ALU.max,
                accum_out=(top_half if u == 0 else top)[:, i : i + 1],
            )

        def look(i):
            nc.scalar.activation(bias[:, i : i + 1], top[:, i : i + 1], ACT.Copy, scale=neg_temp_col[:, i : i + 1])
            looks[i] = ring.tile([P, M], F32, name="look")
            nc.scalar.activation(
                looks[i][:], e_tiles[i][:].indirect(pos1_sb[:]), ACT.Exp,
                bias=bias[:, i : i + 1], scale=temp_col[:, i : i + 1],
            )

        def pick(i):
            picks[i] = ring.tile([P, M], F32, name="pick", bufs=4)
            nc.vector.tensor_copy(picks[i][:], e_tiles[i][:].indirect(pos2_sb[:]))

        def weigh(i):
            g, t = divmod(i, PACK)
            weights[i] = ring.tile([P, M], F32, name="weights")
            nc.scalar.activation(weights[i][:], signs_sb[g][:, t, :], ACT.Copy, scale=gain_col[:, i : i + 1])

        def sign(i):
            signed[i] = ring.tile([P, M], F32, name="signed")
            engine = nc.vector if i == tiles - 1 else nc.gpsimd
            engine.tensor_tensor(signed[i][:], looks[i][:], weights[i][:], ALU.mult)

        def cap(i, cols):
            g, t = divmod(i, PACK)
            nc.vector.scalar_tensor_tensor(
                y[g][:, t, cols], picks[i][:, cols], gain_col[:, i : i + 1], signed[i][:, cols], ALU.mult, ALU.min
            )

        def store_rows(i):
            g, t = divmod(i, PACK)
            rows = out_0[g * GROUP : (g + 1) * GROUP, :].rearrange("(p t) m -> p t m", t=PACK)
            nc.sync.dma_start(out=rows[:, t, :], in_=y[g][:, t, :])

        def round_page(g, cols, rounded, first, copy):
            copy(
                out=rounded[:, PACK * (cols.start - first) : PACK * (cols.stop - first)].rearrange(
                    "p (c i t) -> p c t i", i=4, t=PACK
                ),
                in_=y[g][:, :, cols].rearrange("p t (c i) -> p c t i", i=4),
            )

        def quantize_page(g, cols, rounded):
            width = cols.stop - cols.start
            codes = held([P, width], U32, "y_codes%d_%d" % (g, cols.start))
            nc.vector.quantize_mx(out=codes[:].bitcast(FP8X4), scales=y_plane[:, g, cols], in_=rounded[:])
            nc.sync.dma_start(
                out=out_1[g].rearrange("p m t -> p (m t)").bitcast(I32)[:, cols], in_=codes[:].bitcast(I32)
            )

        whole, left, right = slice(0, M), slice(0, M // 2), slice(M // 2, M)
        last = tiles - 1
        first_page = held([P, PACK * M], BF16, "first_page")
        left_page = held([P, PACK * M // 2], BF16, "left_page")
        right_page = held([P, PACK * M // 2], BF16, "right_page")
        scores(0, 0)
        quantize_h(h_right, BANK // 2)
        weigh(0)
        for i in range(tiles):
            scores(i, 1)
            look(i)
            if i < last:
                sign(i)
                weigh(i + 1)
                scores(i + 1, 0)
            if i > 1:
                cap(i - 2, whole)
                store_rows(i - 2)
            if i == 1:
                wa_mx.append(quantize(wa_rounded[1], "wa_1"))
            pick(i)
            if i in (PACK + 1, PACK + 2):
                round_page(0, left if i == PACK + 1 else right, first_page, 0, nc.scalar.copy)
        cap(last - 1, whole)
        store_rows(last - 1)
        quantize_page(0, whole, first_page)
        sign(last)
        cap(last, left)
        round_page(1, left, left_page, left.start, nc.scalar.copy)
        cap(last, right)
        store_rows(last)
        round_page(1, right, right_page, right.start, nc.vector.tensor_copy)
        quantize_page(1, right, right_page)
        quantize_page(1, left, left_page)
        for q in range(QUADS):
            queue = nc.sync if q % 2 == 0 else nc.scalar
            queue.dma_start(
                out=out_2[:, 4 * q : 4 * q + 4, :].rearrange("g r m -> r g m").bitcast(I32),
                in_=y_plane[32 * q : 32 * q + 4, :, :].bitcast(I32),
            )
